import numpy as np
import ml_dtypes


def mxq(x, axis, fmt="e4m3"):
    dtype, down = {"e4m3": (ml_dtypes.float8_e4m3fn, 7), "e5m2": (ml_dtypes.float8_e5m2, 14)}[fmt]
    v = np.moveaxis(np.asarray(x, np.float32).astype(ml_dtypes.bfloat16).astype(np.float64), axis, -1)
    blocks = v.reshape(v.shape[:-1] + (-1, 32))
    amax = np.abs(blocks).max(-1, keepdims=True)
    byte = np.maximum(np.where(amax > 0, np.frexp(amax)[1] - 1 + 127, 0) - down, 1)
    scale = np.exp2(byte - 127.0)
    codes = (blocks / scale).astype(np.float32).astype(dtype).astype(np.float64)
    return np.moveaxis((codes * scale).reshape(v.shape), -1, axis)


WIDE = False


def mx_kscale(k):
    if not WIDE:
        return np.ones(k)
    levels = np.array([10, -10, 5, -5, 0])
    if k % 512:
        return np.exp2(np.random.permutation(np.resize(levels, k // 32))).repeat(32)
    a = np.empty((k // 512, 16))
    for p in range(k // 512):
        a[p, :8] = np.random.permutation(np.resize(levels, 8))
        for g in range(8):
            far = levels[np.abs(levels - a[p, g]) >= 10]
            a[p, g + 8] = far[np.random.randint(len(far))]
    return np.exp2(a.ravel()).repeat(32)


def f64(x):
    return np.asarray(x).astype(np.float64)


def striped(idx):
    return np.tile(idx.reshape(-1, 16).T, (8, 1)).astype(np.uint16)


def unstriped(offs):
    return offs[:16].T.reshape(-1).astype(np.int64)


def pack_weight(w):
    k, n = w.shape
    w = f64(np.asarray(w, np.float32).astype(ml_dtypes.bfloat16)).reshape(k // 32, 32, n)
    amax = np.abs(w).max(1)
    byte = np.clip(np.where(amax > 0, np.frexp(amax)[1] - 1 + 127 - 7, 1), 1, 254)
    scaled = (w * np.exp2(127.0 - byte)[:, None, :]).reshape(k, n).astype(np.float32)
    words = np.ascontiguousarray(scaled.reshape(k // 512, 128, 4, n).transpose(0, 1, 3, 2)).astype(ml_dtypes.float8_e4m3fn).view(np.uint8)
    return words, np.ascontiguousarray(byte.astype(np.uint8).reshape(k // 512, 16, n))


def unpack_weight(words, scales):
    g, p, n, _ = words.shape
    vals = np.ascontiguousarray(words).view(ml_dtypes.float8_e4m3fn).astype(np.float64) * np.repeat(np.exp2(scales.astype(np.float64) - 127.0), 8, axis=1)[..., None]
    return vals.transpose(0, 1, 3, 2).reshape(g * 512, n)


K, T, S, N, U = 1024, 1024, 512, 128, 512
P = 2 ** 7


def setup_inputs():
    n = np.random.standard_normal
    s = mx_kscale(K)[:, None]
    packed_xT = pack_weight(n((K, T)) * s)
    return {
        "x_words": packed_xT[0],
        "x_scales": packed_xT[1],
        "w1": (n((K, N)) / np.sqrt(K) / s).astype(np.float32),
        "pipe": (np.tile(np.random.uniform(0.5, 1.5, U), (P, 1))).astype(np.float32),
        "offs": striped(np.random.permutation(T)[:S]),
        "fr": striped(np.random.randint(0, S, U)),
        "to": striped(np.random.randint(0, S, U)),
    }


def reference(x_words, x_scales, w1, pipe, offs, fr, to):
    xq = unpack_weight(x_words, x_scales)[:, unstriped(offs)]
    y = mxq(f64(w1), 0, "e4m3").T @ xq
    pres = np.log(np.exp(y) + 1.0) + 0.3
    dp = (pres[:, unstriped(fr)]) ** 2 - ((pres[:, unstriped(to)]) ** 2)
    flow = (f64(pipe)[:1] * dp) / (np.sqrt(np.abs(dp) + 0.1))
    return 0.5 * (np.log(np.exp(2.0 * flow) + 1.0)) + 0.7 * (pres[:, unstriped(to)] / pres[:, unstriped(fr)])

@@ -1,0 +1,175 @@
+import math
+from contextlib import ExitStack
+
+import concourse.mybir as mybir
+
+F32 = mybir.dt.float32
+BF16 = mybir.dt.bfloat16
+I32 = mybir.dt.int32
+U32 = mybir.dt.uint32
+U16 = mybir.dt.uint16
+U8 = mybir.dt.uint8
+FP8X4 = mybir.dt.float8_e4m3fn_x4
+ACT = mybir.ActivationFunctionType
+ALU = mybir.AluOpType
+
+P = 128
+PASSES = 2
+T = 1024
+S = 512
+U = 512
+M = 128
+FLOPS = 2 * 1024 * M * S
+CLAMP = 30.0
+RAT_A = True
+X_ON_S = False
+SQ_V = []
+LN_T4 = (-3.0032631233886042, -1.3553527221278168, -0.5253784487427468, -0.09881458506001962)
+WEIGHT4 = (2.5633502331761955, 1.101830323580734, 0.6067330590728673, 0.2537775212095761)
+NODE_CHUNKS = [128,128,128,128]
+PIPE_CHUNKS = [256,256]
+OUT_CHUNKS = [256,256]
+LN_T = (-2.5028719472704886, -0.8787850595833798, -0.1627327279747613)
+WEIGHT = (2.5582477049910053, 1.0474676363541973, 0.4184521508275042)
+
+
+def spans(widths):
+    result, start = [], 0
+    for width in widths:
+        result.append(slice(start, start + width))
+        start += width
+    return result
+
+
+def cols16(span):
+    return slice(span.start // 16, span.stop // 16)
+
+
+def tile_picked_yweymth_comp_p_kernel(tc, x_words, x_scales, w1, pipe, offs, fr, to, out):
+    nc = tc.nc
+    with ExitStack() as ctx:
+        lists = ctx.enter_context(tc.tile_pool(name="lists", bufs=1))
+        keep = ctx.enter_context(tc.tile_pool(name="keep", bufs=1))
+        psum = ctx.enter_context(tc.psum_pool(name="psum", bufs=1))
+
+        offs_t = lists.tile([P, S // 16], U16, name="offs_t")
+        fr_t = lists.tile([P, U // 16], U16, name="fr_t")
+        to_t = lists.tile([P, U // 16], U16, name="to_t")
+
+        scale_table = keep.tile([P, T], U8, name="scale_table", align_bytes=64)
+        nc.vector.memset(scale_table[:].bitcast(I32), 0)
+        short = keep.tile([P, S + 8], F32, name="short")
+        nc.vector.memset(short[:, S : S + 8], -42.0)
+        w_raw = [keep.tile([P, 4, M], F32, name=f"w_raw{o}", tag=f"stage{o}") for o in range(PASSES)]
+        w_rows = w1.rearrange("(o p j) m -> o p j m", o=PASSES, j=4)
+
+        nc.sync.dma_start(offs_t[:], offs)
+        word_table = [keep.tile([P, T], U32, name=f"word_table{o}", align_bytes=64) for o in range(PASSES)]
+
+        def load_words(o):
+            nc.sync.dma_start(out=word_table[o][:].bitcast(I32), in_=x_words[o].rearrange("p n t -> p (n t)").bitcast(I32))
+
+        load_words(0)
+        for q in range(4):
+            queue = nc.sync if q < 2 else nc.scalar
+            queue.dma_start(out=scale_table[32 * q : 32 * q + 8, :].bitcast(I32), in_=x_scales[:, 4 * q : 4 * q + 4, :].bitcast(I32))
+        nc.sync.dma_start(out=w_raw[0][:], in_=w_rows[0])
+        nc.sync.dma_start(out=w_raw[1][:], in_=w_rows[1])
+        if RAT_A:
+            warm = keep.tile([P, 1], F32, name="warm")
+            nc.scalar.activation(warm[:], short[:, S : S + 1], ACT.Sigmoid)
+        load_words(1)
+        nc.sync.dma_start(fr_t[:], fr)
+        nc.sync.dma_start(to_t[:], to)
+
+        x_code = [keep.tile([P, S], U32, name=f"x_code{o}", align_bytes=64) for o in range(PASSES)]
+        nc.vector.tensor_copy(x_code[0][:], word_table[0][:].indirect(offs_t[:]))
+        x_scale = keep.tile([P, S], U8, name="x_scale", align_bytes=64)
+        nc.vector.tensor_copy(x_scale[:], scale_table[:].indirect(offs_t[:]))
+        w_code, w_scale = [None, None], [None, None]
+        for o in range(PASSES):
+            grouped = keep.tile([P, M, 4], BF16, name=f"grouped{o}", align_bytes=64)
+            cast = nc.scalar.copy
+            cast(out=grouped[:].rearrange("p (c i) t -> p c t i", i=4), in_=w_raw[o][:].rearrange("p t (c i) -> p c t i", i=4))
+            w_code[o] = keep.tile([P, M], U32, name=f"w_code{o}", align_bytes=64)
+            w_scale[o] = keep.tile([P, M], U8, name=f"w_scale{o}", align_bytes=64)
+            nc.vector.quantize_mx(out=w_code[o][:].bitcast(FP8X4), scales=w_scale[o][:], in_=grouped[:].rearrange("p m t -> p (m t)"))
+        pipe_t = keep.tile([P, U], F32, name="pipe_t", tag="stage1")
+        nc.sync.dma_start(out=pipe_t[:], in_=pipe)
+
+        node_spans = spans(NODE_CHUNKS)
+        y = [psum.tile([P, span.stop - span.start], F32, name=f"y{c}") for c, span in enumerate(node_spans)]
+
+        def product(o, c):
+            span = node_spans[c]
+            nc.tensor.matmul_mx(out=y[c][:], lhsT=w_code[o][:].bitcast(FP8X4), lhsT_scale=w_scale[o][:],
+                                rhs=x_code[o][:, span].bitcast(FP8X4), rhs_scale=x_scale[4 * o : P, span],
+                                start=(o == 0), stop=(o == PASSES - 1))
+
+        for c in range(len(node_spans)):
+            product(0, c)
+        pres = keep.tile([P, S], F32, name="pres")
+        pres_sq = keep.tile([P, S], F32, name="pres_sq")
+        for c, span in enumerate(node_spans):
+            nc.vector.tensor_copy(x_code[1][:, span], word_table[1][:].indirect(offs_t[:, cols16(span)]))
+            product(1, c)
+        sig = keep.tile([P, S], F32, name="sig")
+        lifted = keep.tile([P, S], F32, name="lifted")
+        soft = keep.tile([P, S], F32, name="soft")
+        for c, span in enumerate(node_spans):
+            nc.scalar.activation(sig[:, span], y[c][:], ACT.Sigmoid, scale=-1.0)
+        for c, span in enumerate(node_spans):
+            nc.vector.tensor_scalar(lifted[:, span], y[c][:], 0.3, None, ALU.add)
+        sq_spans = spans([128,128,128,128])
+        for span in sq_spans:
+            nc.scalar.activation(soft[:, span], sig[:, span], ACT.Ln, bias=warm[:], scale=math.exp(-0.3))
+            nc.vector.scalar_tensor_tensor(pres[:, span], soft[:, span], -1.0, lifted[:, span], ALU.mult, ALU.max)
+        for c, span in enumerate(sq_spans):
+            if c in SQ_V:
+                nc.vector.tensor_tensor(pres_sq[:, span], pres[:, span], pres[:, span], ALU.mult)
+            else:
+                nc.scalar.activation(pres_sq[:, span], pres[:, span], ACT.Square)
+
+        names = ("sq_fr", "drop", "inv_fr", "ratio", "scaled", "flow", "arg", "rest", "t0", "t1", "t2", "acc0", "acc1", "res")
+        t = {name: keep.tile([P, U], F32, name=name) for name in names}
+        mag = keep.tile([P, U + 8], F32, name="mag")
+        inv_root = keep.tile([P, U + 8], F32, name="inv_root")
+        if X_ON_S:
+            nc.gpsimd.memset(mag[:, U : U + 8], 0.0)
+        pipe_spans = spans(PIPE_CHUNKS)
+        for span in pipe_spans:
+            nc.vector.tensor_copy(t["sq_fr"][:, span], pres_sq[:].indirect(fr_t[:, cols16(span)]))
+        for span in pipe_spans:
+            nc.vector.tensor_tensor(t["drop"][:, span], pres_sq[:].indirect(to_t[:, cols16(span)]), t["sq_fr"][:, span], ALU.subtract)
+        for span in pipe_spans:
+            nc.scalar.activation(t["inv_fr"][:, span], t["sq_fr"][:, span], ACT.Abs_reciprocal_sqrt, scale=1.0 / 0.49)
+        for span in pipe_spans:
+            nc.scalar.activation(mag[:, span], t["drop"][:, span], ACT.Abs)
+            wide = slice(span.start, span.stop + (8 if span.stop == U and X_ON_S else 0))
+            nc.scalar.activation(inv_root[:, wide], mag[:, wide], ACT.Abs_reciprocal_sqrt, bias=0.1)
+        for span in pipe_spans[:0]:
+            nc.scalar.activation(t["inv_fr"][:, span], t["sq_fr"][:, span], ACT.Abs_reciprocal_sqrt, scale=1.0 / 0.49)
+        for span in pipe_spans:
+            nc.vector.tensor_tensor(t["scaled"][:, span], t["drop"][:, span], pipe_t[:, span], ALU.mult)
+        for span in pipe_spans:
+            nc.vector.scalar_tensor_tensor(t["flow"][:, span], t["scaled"][:, span], -1.0, inv_root[:, span], ALU.mult, ALU.mult)
+        out_spans = spans(OUT_CHUNKS)
+        if X_ON_S:
+            half = keep.tile([P, 1], F32, name="half")
+            nc.scalar.activation(half[:], inv_root[:, U : U + 1], ACT.Sigmoid, scale=0.0)
+            for span in out_spans:
+                nc.scalar.activation(t["arg"][:, span], t["flow"][:, span], ACT.Abs, scale=half[:])
+        else:
+            for span in pipe_spans:
+                nc.vector.scalar_tensor_tensor(t["arg"][:, span], t["flow"][:, span], -1.0, t["flow"][:, span], ALU.mult, ALU.max)
+        for span in out_spans:
+            nc.vector.tensor_tensor(t["ratio"][:, span], pres[:].indirect(to_t[:, cols16(span)]), t["inv_fr"][:, span], ALU.mult)
+        for span in out_spans:
+            nc.vector.scalar_tensor_tensor(t["rest"][:, span], t["flow"][:, span], 0.0, t["ratio"][:, span], ALU.max, ALU.add)
+        chain = ("rest", "acc0", "acc1", "res")
+        for i in range(3):
+            for span in out_spans:
+                nc.scalar.activation(t[f"t{i}"][:, span], t["arg"][:, span], ACT.Sigmoid, bias=LN_T[i], scale=-4.0 if X_ON_S else -2.0)
+                nc.vector.scalar_tensor_tensor(t[chain[i + 1]][:, span], t[f"t{i}"][:, span], 0.5 * WEIGHT[i], t[chain[i]][:, span], ALU.mult, ALU.add)
+        for span in out_spans:
+            nc.sync.dma_start(out=out[:, span], in_=t["res"][:, span])

@@ -71,7 +71,7 @@ def tile_picked_yweymth_comp_p_kernel(tc, x_words, x_scales, w1, pipe, offs, fr,
 
         load_words(0)
         for q in range(4):
-            queue = nc.sync if q < 2 else nc.scalar
+            queue = nc.sync
             queue.dma_start(out=scale_table[32 * q : 32 * q + 8, :].bitcast(I32), in_=x_scales[:, 4 * q : 4 * q + 4, :].bitcast(I32))
         nc.sync.dma_start(out=w_raw[0][:], in_=w_rows[0])
         nc.sync.dma_start(out=w_raw[1][:], in_=w_rows[1])

import math
from contextlib import ExitStack

import concourse.mybir as mybir

F32 = mybir.dt.float32
BF16 = mybir.dt.bfloat16
I32 = mybir.dt.int32
U32 = mybir.dt.uint32
U16 = mybir.dt.uint16
U8 = mybir.dt.uint8
FP8X4 = mybir.dt.float8_e4m3fn_x4
ACT = mybir.ActivationFunctionType
ALU = mybir.AluOpType

P = 128
PASSES = 2
T = 1024
S = 512
U = 512
M = 128
FLOPS = 2 * 1024 * M * S
CLAMP = 30.0
RAT_A = True
X_ON_S = False
SQ_V = []
LN_T4 = (-3.0032631233886042, -1.3553527221278168, -0.5253784487427468, -0.09881458506001962)
WEIGHT4 = (2.5633502331761955, 1.101830323580734, 0.6067330590728673, 0.2537775212095761)
NODE_CHUNKS = [128,128,128,128]
PIPE_CHUNKS = [256,256]
OUT_CHUNKS = [256,256]
LN_T = (-2.5028719472704886, -0.8787850595833798, -0.1627327279747613)
WEIGHT = (2.5582477049910053, 1.0474676363541973, 0.4184521508275042)


def spans(widths):
    result, start = [], 0
    for width in widths:
        result.append(slice(start, start + width))
        start += width
    return result


def cols16(span):
    return slice(span.start // 16, span.stop // 16)


def tile_picked_yweymth_comp_p_kernel(tc, x_words, x_scales, w1, pipe, offs, fr, to, out):
    nc = tc.nc
    with ExitStack() as ctx:
        lists = ctx.enter_context(tc.tile_pool(name="lists", bufs=1))
        keep = ctx.enter_context(tc.tile_pool(name="keep", bufs=1))
        psum = ctx.enter_context(tc.psum_pool(name="psum", bufs=1))

        offs_t = lists.tile([P, S // 16], U16, name="offs_t")
        fr_t = lists.tile([P, U // 16], U16, name="fr_t")
        to_t = lists.tile([P, U // 16], U16, name="to_t")

        scale_table = keep.tile([P, T], U8, name="scale_table", align_bytes=64)
        nc.vector.memset(scale_table[:].bitcast(I32), 0)
        short = keep.tile([P, S + 8], F32, name="short")
        nc.vector.memset(short[:, S : S + 8], -42.0)
        w_raw = [keep.tile([P, 4, M], F32, name=f"w_raw{o}", tag=f"stage{o}") for o in range(PASSES)]
        w_rows = w1.rearrange("(o p j) m -> o p j m", o=PASSES, j=4)

        nc.sync.dma_start(offs_t[:], offs)
        word_table = [keep.tile([P, T], U32, name=f"word_table{o}", align_bytes=64) for o in range(PASSES)]

        def load_words(o):
            nc.sync.dma_start(out=word_table[o][:].bitcast(I32), in_=x_words[o].rearrange("p n t -> p (n t)").bitcast(I32))

        load_words(0)
        for q in range(4):
            queue = nc.sync
            queue.dma_start(out=scale_table[32 * q : 32 * q + 8, :].bitcast(I32), in_=x_scales[:, 4 * q : 4 * q + 4, :].bitcast(I32))
        nc.sync.dma_start(out=w_raw[0][:], in_=w_rows[0])
        nc.sync.dma_start(out=w_raw[1][:], in_=w_rows[1])
        if RAT_A:
            warm = keep.tile([P, 1], F32, name="warm")
            nc.scalar.activation(warm[:], short[:, S : S + 1], ACT.Sigmoid)
        load_words(1)
        nc.sync.dma_start(fr_t[:], fr)
        nc.sync.dma_start(to_t[:], to)

        x_code = [keep.tile([P, S], U32, name=f"x_code{o}", align_bytes=64) for o in range(PASSES)]
        nc.vector.tensor_copy(x_code[0][:], word_table[0][:].indirect(offs_t[:]))
        x_scale = keep.tile([P, S], U8, name="x_scale", align_bytes=64)
        nc.vector.tensor_copy(x_scale[:], scale_table[:].indirect(offs_t[:]))
        w_code, w_scale = [None, None], [None, None]
        for o in range(PASSES):
            grouped = keep.tile([P, M, 4], BF16, name=f"grouped{o}", align_bytes=64)
            cast = nc.scalar.copy
            cast(out=grouped[:].rearrange("p (c i) t -> p c t i", i=4), in_=w_raw[o][:].rearrange("p t (c i) -> p c t i", i=4))
            w_code[o] = keep.tile([P, M], U32, name=f"w_code{o}", align_bytes=64)
            w_scale[o] = keep.tile([P, M], U8, name=f"w_scale{o}", align_bytes=64)
            nc.vector.quantize_mx(out=w_code[o][:].bitcast(FP8X4), scales=w_scale[o][:], in_=grouped[:].rearrange("p m t -> p (m t)"))
        pipe_t = keep.tile([P, U], F32, name="pipe_t", tag="stage1")
        nc.sync.dma_start(out=pipe_t[:], in_=pipe)

        node_spans = spans(NODE_CHUNKS)
        y = [psum.tile([P, span.stop - span.start], F32, name=f"y{c}") for c, span in enumerate(node_spans)]

        def product(o, c):
            span = node_spans[c]
            nc.tensor.matmul_mx(out=y[c][:], lhsT=w_code[o][:].bitcast(FP8X4), lhsT_scale=w_scale[o][:],
                                rhs=x_code[o][:, span].bitcast(FP8X4), rhs_scale=x_scale[4 * o : P, span],
                                start=(o == 0), stop=(o == PASSES - 1))

        for c in range(len(node_spans)):
            product(0, c)
        pres = keep.tile([P, S], F32, name="pres")
        pres_sq = keep.tile([P, S], F32, name="pres_sq")
        for c, span in enumerate(node_spans):
            nc.vector.tensor_copy(x_code[1][:, span], word_table[1][:].indirect(offs_t[:, cols16(span)]))
            product(1, c)
        sig = keep.tile([P, S], F32, name="sig")
        lifted = keep.tile([P, S], F32, name="lifted")
        soft = keep.tile([P, S], F32, name="soft")
        for c, span in enumerate(node_spans):
            nc.scalar.activation(sig[:, span], y[c][:], ACT.Sigmoid, scale=-1.0)
        for c, span in enumerate(node_spans):
            nc.vector.tensor_scalar(lifted[:, span], y[c][:], 0.3, None, ALU.add)
        sq_spans = spans([128,128,128,128])
        for span in sq_spans:
            nc.scalar.activation(soft[:, span], sig[:, span], ACT.Ln, bias=warm[:], scale=math.exp(-0.3))
            nc.vector.scalar_tensor_tensor(pres[:, span], soft[:, span], -1.0, lifted[:, span], ALU.mult, ALU.max)
        for c, span in enumerate(sq_spans):
            if c in SQ_V:
                nc.vector.tensor_tensor(pres_sq[:, span], pres[:, span], pres[:, span], ALU.mult)
            else:
                nc.scalar.activation(pres_sq[:, span], pres[:, span], ACT.Square)

        names = ("sq_fr", "drop", "inv_fr", "ratio", "scaled", "flow", "arg", "rest", "t0", "t1", "t2", "acc0", "acc1", "res")
        t = {name: keep.tile([P, U], F32, name=name) for name in names}
        mag = keep.tile([P, U + 8], F32, name="mag")
        inv_root = keep.tile([P, U + 8], F32, name="inv_root")
        if X_ON_S:
            nc.gpsimd.memset(mag[:, U : U + 8], 0.0)
        pipe_spans = spans(PIPE_CHUNKS)
        for span in pipe_spans:
            nc.vector.tensor_copy(t["sq_fr"][:, span], pres_sq[:].indirect(fr_t[:, cols16(span)]))
        for span in pipe_spans:
            nc.vector.tensor_tensor(t["drop"][:, span], pres_sq[:].indirect(to_t[:, cols16(span)]), t["sq_fr"][:, span], ALU.subtract)
        for span in pipe_spans:
            nc.scalar.activation(t["inv_fr"][:, span], t["sq_fr"][:, span], ACT.Abs_reciprocal_sqrt, scale=1.0 / 0.49)
        for span in pipe_spans:
            nc.scalar.activation(mag[:, span], t["drop"][:, span], ACT.Abs)
            wide = slice(span.start, span.stop + (8 if span.stop == U and X_ON_S else 0))
            nc.scalar.activation(inv_root[:, wide], mag[:, wide], ACT.Abs_reciprocal_sqrt, bias=0.1)
        for span in pipe_spans[:0]:
            nc.scalar.activation(t["inv_fr"][:, span], t["sq_fr"][:, span], ACT.Abs_reciprocal_sqrt, scale=1.0 / 0.49)
        for span in pipe_spans:
            nc.vector.tensor_tensor(t["scaled"][:, span], t["drop"][:, span], pipe_t[:, span], ALU.mult)
        for span in pipe_spans:
            nc.vector.scalar_tensor_tensor(t["flow"][:, span], t["scaled"][:, span], -1.0, inv_root[:, span], ALU.mult, ALU.mult)
        out_spans = spans(OUT_CHUNKS)
        if X_ON_S:
            half = keep.tile([P, 1], F32, name="half")
            nc.scalar.activation(half[:], inv_root[:, U : U + 1], ACT.Sigmoid, scale=0.0)
            for span in out_spans:
                nc.scalar.activation(t["arg"][:, span], t["flow"][:, span], ACT.Abs, scale=half[:])
        else:
            for span in pipe_spans:
                nc.vector.scalar_tensor_tensor(t["arg"][:, span], t["flow"][:, span], -1.0, t["flow"][:, span], ALU.mult, ALU.max)
        for span in out_spans:
            nc.vector.tensor_tensor(t["ratio"][:, span], pres[:].indirect(to_t[:, cols16(span)]), t["inv_fr"][:, span], ALU.mult)
        for span in out_spans:
            nc.vector.scalar_tensor_tensor(t["rest"][:, span], t["flow"][:, span], 0.0, t["ratio"][:, span], ALU.max, ALU.add)
        chain = ("rest", "acc0", "acc1", "res")
        for i in range(3):
            for span in out_spans:
                nc.scalar.activation(t[f"t{i}"][:, span], t["arg"][:, span], ACT.Sigmoid, bias=LN_T[i], scale=-4.0 if X_ON_S else -2.0)
                nc.vector.scalar_tensor_tensor(t[chain[i + 1]][:, span], t[f"t{i}"][:, span], 0.5 * WEIGHT[i], t[chain[i]][:, span], ALU.mult, ALU.add)
        for span in out_spans:
            nc.sync.dma_start(out=out[:, span], in_=t["res"][:, span])
